import numpy as np
import ml_dtypes


def mxq(x, axis, fmt="e4m3"):
    dtype, down = {"e4m3": (ml_dtypes.float8_e4m3fn, 7), "e5m2": (ml_dtypes.float8_e5m2, 14)}[fmt]
    v = np.moveaxis(np.asarray(x, np.float32).astype(ml_dtypes.bfloat16).astype(np.float64), axis, -1)
    blocks = v.reshape(v.shape[:-1] + (-1, 32))
    amax = np.abs(blocks).max(-1, keepdims=True)
    byte = np.maximum(np.where(amax > 0, np.frexp(amax)[1] - 1 + 127, 0) - down, 1)
    scale = np.exp2(byte - 127.0)
    codes = (blocks / scale).astype(np.float32).astype(dtype).astype(np.float64)
    return np.moveaxis((codes * scale).reshape(v.shape), -1, axis)


WIDE = False


def mx_kscale(k):
    if not WIDE:
        return np.ones(k)
    levels = np.array([10, -10, 5, -5, 0])
    if k % 512:
        return np.exp2(np.random.permutation(np.resize(levels, k // 32))).repeat(32)
    a = np.empty((k // 512, 16))
    for p in range(k // 512):
        a[p, :8] = np.random.permutation(np.resize(levels, 8))
        for g in range(8):
            far = levels[np.abs(levels - a[p, g]) >= 10]
            a[p, g + 8] = far[np.random.randint(len(far))]
    return np.exp2(a.ravel()).repeat(32)


def f64(x):
    return np.asarray(x).astype(np.float64)


def striped(idx):
    return np.tile(idx.reshape(-1, 16).T, (8, 1)).astype(np.uint16)


def unstriped(offs):
    return offs[:16].T.reshape(-1).astype(np.int64)


E2M1 = np.array([0.0, 0.5, 1.0, 1.5, 2.0, 3.0, 4.0, 6.0, -0.0, -0.5, -1.0, -1.5, -2.0, -3.0, -4.0, -6.0])


def pack_weight(w, fmt):
    k, n = w.shape
    w = f64(np.asarray(w, np.float32).astype(ml_dtypes.bfloat16)).reshape(k // 32, 32, n)
    amax = np.abs(w).max(1)
    if fmt == "e4m3":
        byte = np.frexp(amax)[1] - 1 + 127 - 7
    else:
        mant, ex = np.frexp(amax / 6.0)
        byte = np.where(mant > 0.5, ex, ex - 1) + 127
    byte = np.clip(np.where(amax > 0, byte, 1), 1, 254)
    scaled = (w * np.exp2(127.0 - byte)[:, None, :]).reshape(k, n).astype(np.float32)
    by_word = np.ascontiguousarray(scaled.reshape(k // 512, 128, 4, n).transpose(0, 1, 3, 2))
    if fmt == "e4m3":
        words = by_word.astype(ml_dtypes.float8_e4m3fn).view(np.uint8)
    else:
        c = by_word.astype(ml_dtypes.float4_e2m1fn).view(np.uint8) & 0xF
        words = (c[..., 0::2] | (c[..., 1::2] << 4)).reshape(k // 512, 128, 2 * n)
    return np.ascontiguousarray(words), np.ascontiguousarray(byte.astype(np.uint8).reshape(k // 512, 16, n))


def unpack_weight(words, scales, fmt):
    g, _, n = scales.shape
    words = np.ascontiguousarray(words).reshape(g, 128, n, -1)
    if fmt == "e4m3":
        vals = words.view(ml_dtypes.float8_e4m3fn).astype(np.float64)
    else:
        nib = np.empty((g, 128, n, 4), np.uint8)
        nib[..., 0::2] = words & 0xF
        nib[..., 1::2] = words >> 4
        vals = E2M1[nib]
    vals = vals * np.repeat(np.exp2(scales.astype(np.float64) - 127.0), 8, axis=1)[..., None]
    return vals.transpose(0, 1, 3, 2).reshape(g * 512, n)


def pack_table(v):
    words, scales = pack_weight(v, "e4m3")
    return np.concatenate([words.reshape(words.shape[0], -1), scales.reshape(scales.shape[0], -1)], axis=1)


def unpack_table(tab):
    g, t = tab.shape[0], tab.shape[1] // 528
    return unpack_weight(tab[:, :512 * t].reshape(g, 128, t, 4), tab[:, 512 * t:].reshape(g, 16, t), "e4m3")


def split(x):
    m, e = np.frexp(f64(x))
    hi = np.ldexp(np.trunc(16.0 * m) / 16.0, e)
    return hi, f64(x) - hi


K, M, T, S = 512, 128, 4096, 1024


def setup_inputs():
    n = np.random.standard_normal
    s = mx_kscale(K)[:, None]
    return {
        "tab": pack_table(n((K, T)) * s),
        "w": (n((K, M)) / np.sqrt(K) / s).astype(np.float32),
        "offs": striped(np.random.permutation(T)[:S]),
    }


def reference(tab, w, offs):
    tab_ = unpack_table(tab)[:, unstriped(offs)]
    w_hi, w_lo = split(w)
    w_hi_, w_lo_ = mxq(w_hi, 0, "e4m3"), mxq(w_lo, 0, "e4m3")
    y = w_hi_.T @ tab_ + w_lo_.T @ tab_
    return y

@@ -1,0 +1,123 @@
+import concourse.mybir as mybir
+from concourse.masks import make_identity
+
+K, M, T, S = 512, 128, 4096, 1024
+P = 128
+PACK = 4
+LANES = 16
+QUADRANT = 32
+HALF = S // 2
+QUARTER = S // 4
+FIRST = 1536
+WARM = 40
+
+FLOPS = 2 * 2 * K * M * S
+
+F32 = mybir.dt.float32
+BF16 = mybir.dt.bfloat16
+I32 = mybir.dt.int32
+U32 = mybir.dt.uint32
+U16 = mybir.dt.uint16
+U8 = mybir.dt.uint8
+FP8X4 = mybir.dt.float8_e4m3fn_x4
+ALU = mybir.AluOpType
+
+HI_BITS = -(1 << 20)
+
+
+def tile_list_tabw_hl_none_kernel(tc, tab, w, offs, out):
+    nc = tc.nc
+    with (
+        tc.tile_pool(name="keep", bufs=1) as keep,
+        tc.psum_pool(name="psum", bufs=1) as psum,
+    ):
+        offsets = keep.tile([P, S // LANES], U16, name="offsets")
+        w_raw = keep.tile([P, PACK, M], F32, name="w_raw", align_bytes=64)
+        table_words = keep.tile([P, T], I32, name="table_words", align_bytes=64)
+        table_scales = keep.tile([P, T], U8, name="table_scales", align_bytes=64)
+
+        nc.sync.dma_start(w_raw[:], w.rearrange("(p j) n -> p j n", j=PACK))
+        nc.sync.dma_start(offsets[:], offs)
+        word_rows = tab[0, : PACK * P * T].rearrange("(p b) -> p b", p=P).bitcast(I32)
+        nc.sync.dma_start(table_words[:, :FIRST], word_rows[:, :FIRST])
+
+        nc.vector.memset(table_scales[:].bitcast(I32), 0)
+        nc.vector.memset(table_words[:, T - 8 :], 0)
+        scale_rows = tab[0, PACK * P * T :].rearrange("(q t) -> q t", t=T)
+        for r in range(4):
+            nc.sync.dma_start(
+                table_scales[r:P:QUADRANT, :].bitcast(I32),
+                scale_rows[r : K // 32 : 4, :].bitcast(I32),
+            )
+        nc.sync.dma_start(table_words[:, FIRST:], word_rows[:, FIRST:])
+
+        w_hi = keep.tile([P, PACK, M], I32, name="w_hi", align_bytes=64)
+        nc.vector.tensor_scalar(w_hi[:], w_raw[:].bitcast(I32), HI_BITS, None, ALU.bitwise_and)
+        hi_grouped = keep.tile([P, M, PACK], BF16, name="hi_grouped", align_bytes=64)
+        lo_grouped = keep.tile([P, M, PACK], BF16, name="lo_grouped", align_bytes=64)
+        w_hi_f = w_hi[:].bitcast(F32)
+        nc.scalar.copy(hi_grouped[:], w_hi_f.rearrange("p j n -> p n j"))
+        nc.vector.tensor_tensor(
+            lo_grouped[:],
+            w_raw[:].rearrange("p j n -> p n j"),
+            w_hi_f.rearrange("p j n -> p n j"),
+            ALU.subtract,
+        )
+
+        parts = []
+        for name, grouped in (("lo", lo_grouped), ("hi", hi_grouped)):
+            codes = keep.tile([P, M], U32, name=name + "_codes", align_bytes=64)
+            scales = keep.tile([P, M], U8, name=name + "_scales", align_bytes=64)
+            nc.vector.quantize_mx(
+                out=codes[:].bitcast(FP8X4),
+                scales=scales[:],
+                in_=grouped[:].rearrange("p n j -> p (n j)"),
+            )
+            parts.append((codes, scales))
+
+        picked_scales = keep.tile([P, S], U8, name="picked_scales", align_bytes=64)
+        nc.vector.tensor_copy(picked_scales[:], table_scales[:].indirect(offsets[:]))
+
+        identity = keep.tile([P, P], BF16, name="identity")
+        make_identity(nc, identity[:])
+        spare = psum.tile([P, P], BF16, name="spare")
+        flat = lo_grouped[:].rearrange("p n j -> p (n j)")
+        for i in range(WARM):
+            nc.tensor.transpose(spare[:], flat[:, (i % PACK) * P : (i % PACK + 1) * P], identity[:])
+
+        words = table_words[:].bitcast(U32)
+        picked = []
+        for h in range(2):
+            picked_words = keep.tile([P, HALF], U32, name="picked_words%d" % h, align_bytes=64)
+            cols = HALF // LANES
+            nc.vector.tensor_copy(picked_words[:], words.indirect(offsets[:, h * cols : (h + 1) * cols]))
+            picked.append(picked_words)
+
+        def product(h, first, width, name):
+            bank = psum.tile([P, width], F32, name="bank_" + name)
+            for i, (codes, scales) in enumerate(parts):
+                nc.tensor.matmul_mx(
+                    out=bank[:],
+                    lhsT=codes[:].bitcast(FP8X4),
+                    lhsT_scale=scales[:],
+                    rhs=picked[h][:, first : first + width].bitcast(FP8X4),
+                    rhs_scale=picked_scales[:, h * HALF + first : h * HALF + first + width],
+                    start=(i == 0),
+                    stop=(i == 1),
+                )
+            return bank
+
+        bank = product(0, 0, HALF, "a")
+        result = keep.tile([P, HALF], F32, name="result_a")
+        nc.scalar.copy(result[:], bank[:])
+        nc.sync.dma_start(out[:, 0:HALF], result[:])
+
+        bank_b = product(1, 0, QUARTER, "b")
+        result_b = keep.tile([P, QUARTER], F32, name="result_b")
+        nc.vector.tensor_copy(result_b[:], bank_b[:])
+        nc.sync.dma_start(out[:, HALF : HALF + QUARTER], result_b[:])
+
+        bank_c = product(1, QUARTER, QUARTER, "c")
+        result_c = keep.tile([P, QUARTER], F32, name="result_c")
+        nc.scalar.copy(result_c[:], bank_c[:])
+        nc.scalar.dma_start(out[:, HALF + QUARTER : S], result_c[:])

@@ -1,5 +1,4 @@
 import concourse.mybir as mybir
-from concourse.masks import make_identity
 
 K, M, T, S = 512, 128, 4096, 1024
 P = 128
@@ -8,8 +7,10 @@ LANES = 16
 QUADRANT = 32
 HALF = S // 2
 QUARTER = S // 4
-FIRST = 1536
-WARM = 40
+BLOCKS = K // 32
+SPREAD_FIRST = 32
+SPREAD_STEP = 4
+FIRST = 512
 
 FLOPS = 2 * 2 * K * M * S
 
@@ -34,74 +35,71 @@ def tile_list_tabw_hl_none_kernel(tc, tab, w, offs, out):
         offsets = keep.tile([P, S // LANES], U16, name="offsets")
         w_raw = keep.tile([P, PACK, M], F32, name="w_raw", align_bytes=64)
         table_words = keep.tile([P, T], I32, name="table_words", align_bytes=64)
-        table_scales = keep.tile([P, T], U8, name="table_scales", align_bytes=64)
+        table_scales = keep.tile([P, T], U8, name="table_scales", tag="shared", align_bytes=64)
+        plane = keep.tile([P, S], U8, name="plane", align_bytes=64)
+
+        nc.vector.memset(table_scales[:].bitcast(I32), 0)
+        nc.vector.memset(plane[:].bitcast(I32), 0)
 
         nc.sync.dma_start(w_raw[:], w.rearrange("(p j) n -> p j n", j=PACK))
         nc.sync.dma_start(offsets[:], offs)
         word_rows = tab[0, : PACK * P * T].rearrange("(p b) -> p b", p=P).bitcast(I32)
         nc.sync.dma_start(table_words[:, :FIRST], word_rows[:, :FIRST])
 
-        nc.vector.memset(table_scales[:].bitcast(I32), 0)
-        nc.vector.memset(table_words[:, T - 8 :], 0)
         scale_rows = tab[0, PACK * P * T :].rearrange("(q t) -> q t", t=T)
-        for r in range(4):
-            nc.sync.dma_start(
-                table_scales[r:P:QUADRANT, :].bitcast(I32),
-                scale_rows[r : K // 32 : 4, :].bitcast(I32),
-            )
+        last = SPREAD_FIRST + SPREAD_STEP * BLOCKS
+        nc.sync.dma_start(
+            table_scales[SPREAD_FIRST:last:SPREAD_STEP, :].bitcast(I32),
+            scale_rows.bitcast(I32),
+        )
         nc.sync.dma_start(table_words[:, FIRST:], word_rows[:, FIRST:])
 
         w_hi = keep.tile([P, PACK, M], I32, name="w_hi", align_bytes=64)
         nc.vector.tensor_scalar(w_hi[:], w_raw[:].bitcast(I32), HI_BITS, None, ALU.bitwise_and)
-        hi_grouped = keep.tile([P, M, PACK], BF16, name="hi_grouped", align_bytes=64)
-        lo_grouped = keep.tile([P, M, PACK], BF16, name="lo_grouped", align_bytes=64)
+
+        picked_scales = keep.tile([P, S], U8, name="picked_scales", align_bytes=64)
+        nc.vector.tensor_copy(picked_scales[:], table_scales[:].indirect(offsets[:]))
+        for q in range(4):
+            first = SPREAD_FIRST + SPREAD_STEP * 4 * q
+            nc.sync.dma_start(
+                plane[QUADRANT * q : QUADRANT * q + 4, :].bitcast(I32),
+                picked_scales[first : first + SPREAD_STEP * 4 : SPREAD_STEP, :].bitcast(I32),
+            )
+
+        grouped = keep.tile([P, 2, M, PACK], BF16, name="grouped", tag="shared", align_bytes=64)
         w_hi_f = w_hi[:].bitcast(F32)
-        nc.scalar.copy(hi_grouped[:], w_hi_f.rearrange("p j n -> p n j"))
+        nc.scalar.copy(grouped[:, 1], w_hi_f.rearrange("p j n -> p n j"))
         nc.vector.tensor_tensor(
-            lo_grouped[:],
+            grouped[:, 0],
             w_raw[:].rearrange("p j n -> p n j"),
             w_hi_f.rearrange("p j n -> p n j"),
             ALU.subtract,
         )
-
-        parts = []
-        for name, grouped in (("lo", lo_grouped), ("hi", hi_grouped)):
-            codes = keep.tile([P, M], U32, name=name + "_codes", align_bytes=64)
-            scales = keep.tile([P, M], U8, name=name + "_scales", align_bytes=64)
-            nc.vector.quantize_mx(
-                out=codes[:].bitcast(FP8X4),
-                scales=scales[:],
-                in_=grouped[:].rearrange("p n j -> p (n j)"),
-            )
-            parts.append((codes, scales))
-
-        picked_scales = keep.tile([P, S], U8, name="picked_scales", align_bytes=64)
-        nc.vector.tensor_copy(picked_scales[:], table_scales[:].indirect(offsets[:]))
-
-        identity = keep.tile([P, P], BF16, name="identity")
-        make_identity(nc, identity[:])
-        spare = psum.tile([P, P], BF16, name="spare")
-        flat = lo_grouped[:].rearrange("p n j -> p (n j)")
-        for i in range(WARM):
-            nc.tensor.transpose(spare[:], flat[:, (i % PACK) * P : (i % PACK + 1) * P], identity[:])
+        codes = keep.tile([P, 2 * M], U32, name="codes", align_bytes=64)
+        scales = keep.tile([P, 2 * M], U8, name="scales", align_bytes=64)
+        nc.vector.quantize_mx(
+            out=codes[:].bitcast(FP8X4),
+            scales=scales[:],
+            in_=grouped[:].rearrange("p h n j -> p (h n j)"),
+        )
 
         words = table_words[:].bitcast(U32)
         picked = []
         for h in range(2):
-            picked_words = keep.tile([P, HALF], U32, name="picked_words%d" % h, align_bytes=64)
+            picked_words = keep.tile([P, HALF], U32, name="picked_words%d" % h, tag=("shared", "second")[h], align_bytes=64)
             cols = HALF // LANES
             nc.vector.tensor_copy(picked_words[:], words.indirect(offsets[:, h * cols : (h + 1) * cols]))
             picked.append(picked_words)
 
         def product(h, first, width, name):
             bank = psum.tile([P, width], F32, name="bank_" + name)
-            for i, (codes, scales) in enumerate(parts):
+            for i in range(2):
                 nc.tensor.matmul_mx(
                     out=bank[:],
-                    lhsT=codes[:].bitcast(FP8X4),
-                    lhsT_scale=scales[:],
+                    lhsT=codes[:, i * M : (i + 1) * M].bitcast(FP8X4),
+                    lhsT_scale=scales[:, i * M : (i + 1) * M],
                     rhs=picked[h][:, first : first + width].bitcast(FP8X4),
-                    rhs_scale=picked_scales[:, h * HALF + first : h * HALF + first + width],
+                    rhs_scale=plane[:, h * HALF + first : h * HALF + first + width],
                     start=(i == 0),
                     stop=(i == 1),
                 )

@@ -54,8 +54,11 @@ def tile_list_tabw_hl_none_kernel(tc, tab, w, offs, out):
         )
         nc.sync.dma_start(table_words[:, FIRST:], word_rows[:, FIRST:])
 
-        w_hi = keep.tile([P, PACK, M], I32, name="w_hi", align_bytes=64)
-        nc.vector.tensor_scalar(w_hi[:], w_raw[:].bitcast(I32), HI_BITS, None, ALU.bitwise_and)
+        parts = keep.tile([P, 2, PACK, M], F32, name="parts", align_bytes=64)
+        nc.vector.tensor_scalar(parts[:, 1].bitcast(I32), w_raw[:].bitcast(I32), HI_BITS, None, ALU.bitwise_and)
+        nc.vector.tensor_tensor(parts[:, 0], w_raw[:], parts[:, 1], ALU.subtract)
+        grouped = keep.tile([P, 2, M, PACK], BF16, name="grouped", tag="grouped", align_bytes=64)
+        nc.scalar.copy(grouped[:], parts[:].rearrange("p h j n -> p h n j"))
 
         picked_scales = keep.tile([P, S], U8, name="picked_scales", align_bytes=64)
         nc.vector.tensor_copy(picked_scales[:], table_scales[:].indirect(offsets[:]))
@@ -66,16 +69,7 @@ def tile_list_tabw_hl_none_kernel(tc, tab, w, offs, out):
                 picked_scales[first : first + SPREAD_STEP * 4 : SPREAD_STEP, :].bitcast(I32),
             )
 
-        grouped = keep.tile([P, 2, M, PACK], BF16, name="grouped", tag="shared", align_bytes=64)
-        w_hi_f = w_hi[:].bitcast(F32)
-        nc.scalar.copy(grouped[:, 1], w_hi_f.rearrange("p j n -> p n j"))
-        nc.vector.tensor_tensor(
-            grouped[:, 0],
-            w_raw[:].rearrange("p j n -> p n j"),
-            w_hi_f.rearrange("p j n -> p n j"),
-            ALU.subtract,
-        )
-        codes = keep.tile([P, 2 * M], U32, name="codes", align_bytes=64)
+        codes = keep.tile([P, 2 * M], U32, name="codes", tag="shared", align_bytes=64)
         scales = keep.tile([P, 2 * M], U8, name="scales", align_bytes=64)
         nc.vector.quantize_mx(
             out=codes[:].bitcast(FP8X4),
@@ -86,7 +80,7 @@ def tile_list_tabw_hl_none_kernel(tc, tab, w, offs, out):
         words = table_words[:].bitcast(U32)
         picked = []
         for h in range(2):
-            picked_words = keep.tile([P, HALF], U32, name="picked_words%d" % h, tag=("shared", "second")[h], align_bytes=64)
+            picked_words = keep.tile([P, HALF], U32, name="picked_words%d" % h, tag=("grouped", "second")[h], align_bytes=64)
             cols = HALF // LANES
             nc.vector.tensor_copy(picked_words[:], words.indirect(offsets[:, h * cols : (h + 1) * cols]))
             picked.append(picked_words)
@@ -112,10 +106,12 @@ def tile_list_tabw_hl_none_kernel(tc, tab, w, offs, out):
 
         bank_b = product(1, 0, QUARTER, "b")
         result_b = keep.tile([P, QUARTER], F32, name="result_b")
-        nc.vector.tensor_copy(result_b[:], bank_b[:])
-        nc.sync.dma_start(out[:, HALF : HALF + QUARTER], result_b[:])
+        nc.scalar.copy(result_b[:], bank_b[:])
+        nc.scalar.dma_start(out[:, HALF : HALF + QUARTER], result_b[:])
 
-        bank_c = product(1, QUARTER, QUARTER, "c")
         result_c = keep.tile([P, QUARTER], F32, name="result_c")
-        nc.scalar.copy(result_c[:], bank_c[:])
-        nc.scalar.dma_start(out[:, HALF + QUARTER : S], result_c[:])
+        bank_c = product(1, QUARTER, P, "c")
+        nc.vector.tensor_copy(result_c[:, :P], bank_c[:])
+        bank_d = product(1, QUARTER + P, P, "d")
+        nc.vector.tensor_copy(result_c[:, P:], bank_d[:])
+        nc.sync.dma_start(out[:, HALF + QUARTER : S], result_c[:])

@@ -64,7 +64,8 @@ def tile_list_tabw_hl_none_kernel(tc, tab, w, offs, out):
         nc.vector.tensor_copy(picked_scales[:], table_scales[:].indirect(offsets[:]))
         for q in range(4):
             first = SPREAD_FIRST + SPREAD_STEP * 4 * q
-            nc.sync.dma_start(
+            queue = (nc.sync, nc.scalar)[q % 2]
+            queue.dma_start(
                 plane[QUADRANT * q : QUADRANT * q + 4, :].bitcast(I32),
                 picked_scales[first : first + SPREAD_STEP * 4 : SPREAD_STEP, :].bitcast(I32),
             )
@@ -99,19 +100,23 @@ def tile_list_tabw_hl_none_kernel(tc, tab, w, offs, out):
                 )
             return bank
 
-        bank = product(0, 0, HALF, "a")
-        result = keep.tile([P, HALF], F32, name="result_a")
-        nc.scalar.copy(result[:], bank[:])
-        nc.sync.dma_start(out[:, 0:HALF], result[:])
+        for part in range(2):
+            bank = product(0, part * QUARTER, QUARTER, "a%d" % part)
+            result = keep.tile([P, QUARTER], F32, name="result_a%d" % part)
+            nc.scalar.copy(result[:], bank[:])
+            nc.sync.dma_start(out[:, part * QUARTER : (part + 1) * QUARTER], result[:])
 
         bank_b = product(1, 0, QUARTER, "b")
         result_b = keep.tile([P, QUARTER], F32, name="result_b")
-        nc.scalar.copy(result_b[:], bank_b[:])
-        nc.scalar.dma_start(out[:, HALF : HALF + QUARTER], result_b[:])
+        nc.vector.tensor_copy(result_b[:], bank_b[:])
+        nc.sync.dma_start(out[:, HALF : HALF + QUARTER], result_b[:])
 
-        result_c = keep.tile([P, QUARTER], F32, name="result_c")
+        result_c = keep.tile([P, P], F32, name="result_c")
         bank_c = product(1, QUARTER, P, "c")
-        nc.vector.tensor_copy(result_c[:, :P], bank_c[:])
+        nc.scalar.copy(result_c[:], bank_c[:])
+        nc.scalar.dma_start(out[:, S - 2 * P : S - P], result_c[:])
+
+        result_d = keep.tile([P, P], F32, name="result_d")
         bank_d = product(1, QUARTER + P, P, "d")
-        nc.vector.tensor_copy(result_c[:, P:], bank_d[:])
-        nc.sync.dma_start(out[:, HALF + QUARTER : S], result_c[:])
+        nc.vector.tensor_copy(result_d[:], bank_d[:])
+        nc.sync.dma_start(out[:, S - P : S], result_d[:])

@@ -11,6 +11,7 @@ BLOCKS = K // 32
 SPREAD_FIRST = 32
 SPREAD_STEP = 4
 FIRST = 512
+WIDTHS = (256, 256, 128, 128, 128, 128)
 
 FLOPS = 2 * 2 * K * M * S
 
@@ -86,37 +87,29 @@ def tile_list_tabw_hl_none_kernel(tc, tab, w, offs, out):
             nc.vector.tensor_copy(picked_words[:], words.indirect(offsets[:, h * cols : (h + 1) * cols]))
             picked.append(picked_words)
 
-        def product(h, first, width, name):
-            bank = psum.tile([P, width], F32, name="bank_" + name)
-            for i in range(2):
+        def product(group, first, width):
+            h, inside = divmod(first, HALF)
+            bank = psum.tile([P, width], F32, name="bank%d" % group)
+            for step in range(2):
+                i = (step + group) % 2
                 nc.tensor.matmul_mx(
                     out=bank[:],
                     lhsT=codes[:, i * M : (i + 1) * M].bitcast(FP8X4),
                     lhsT_scale=scales[:, i * M : (i + 1) * M],
-                    rhs=picked[h][:, first : first + width].bitcast(FP8X4),
-                    rhs_scale=plane[:, h * HALF + first : h * HALF + first + width],
-                    start=(i == 0),
-                    stop=(i == 1),
+                    rhs=picked[h][:, inside : inside + width].bitcast(FP8X4),
+                    rhs_scale=plane[:, first : first + width],
+                    start=(step == 0),
+                    stop=(step == 1),
                 )
             return bank
 
-        for part in range(2):
-            bank = product(0, part * QUARTER, QUARTER, "a%d" % part)
-            result = keep.tile([P, QUARTER], F32, name="result_a%d" % part)
-            nc.scalar.copy(result[:], bank[:])
-            nc.sync.dma_start(out[:, part * QUARTER : (part + 1) * QUARTER], result[:])
-
-        bank_b = product(1, 0, QUARTER, "b")
-        result_b = keep.tile([P, QUARTER], F32, name="result_b")
-        nc.vector.tensor_copy(result_b[:], bank_b[:])
-        nc.sync.dma_start(out[:, HALF : HALF + QUARTER], result_b[:])
-
-        result_c = keep.tile([P, P], F32, name="result_c")
-        bank_c = product(1, QUARTER, P, "c")
-        nc.scalar.copy(result_c[:], bank_c[:])
-        nc.scalar.dma_start(out[:, S - 2 * P : S - P], result_c[:])
-
-        result_d = keep.tile([P, P], F32, name="result_d")
-        bank_d = product(1, QUARTER + P, P, "d")
-        nc.vector.tensor_copy(result_d[:], bank_d[:])
-        nc.sync.dma_start(out[:, S - P : S], result_d[:])
+        first = 0
+        for group, width in enumerate(WIDTHS):
+            bank = product(group, first, width)
+            result = keep.tile([P, width], F32, name="result%d" % group)
+            if first > HALF and group % 2 == 1:
+                nc.vector.tensor_copy(result[:], bank[:])
+            else:
+                nc.scalar.copy(result[:], bank[:])
+            nc.sync.dma_start(out[:, first : first + width], result[:])
+            first = first + width

@@ -33,11 +33,11 @@ def tile_list_tabw_hl_none_kernel(tc, tab, w, offs, out):
         tc.tile_pool(name="keep", bufs=1) as keep,
         tc.psum_pool(name="psum", bufs=1) as psum,
     ):
-        offsets = keep.tile([P, S // LANES], U16, name="offsets")
-        w_raw = keep.tile([P, PACK, M], F32, name="w_raw", align_bytes=64)
-        table_words = keep.tile([P, T], I32, name="table_words", align_bytes=64)
-        table_scales = keep.tile([P, T], U8, name="table_scales", tag="shared", align_bytes=64)
-        plane = keep.tile([P, S], U8, name="plane", align_bytes=64)
+        offsets = keep.tile([P, S // LANES], U16, name="offsets", align_bytes=256)
+        w_raw = keep.tile([P, PACK, M], F32, name="w_raw", align_bytes=256)
+        table_words = keep.tile([P, T], I32, name="table_words", align_bytes=256)
+        table_scales = keep.tile([P, T], U8, name="table_scales", tag="shared", align_bytes=256)
+        plane = keep.tile([P, S], U8, name="plane", align_bytes=256)
 
         nc.vector.memset(table_scales[:].bitcast(I32), 0)
         nc.vector.memset(plane[:].bitcast(I32), 0)
@@ -55,13 +55,13 @@ def tile_list_tabw_hl_none_kernel(tc, tab, w, offs, out):
         )
         nc.sync.dma_start(table_words[:, FIRST:], word_rows[:, FIRST:])
 
-        parts = keep.tile([P, 2, PACK, M], F32, name="parts", align_bytes=64)
+        parts = keep.tile([P, 2, PACK, M], F32, name="parts", align_bytes=256)
         nc.vector.tensor_scalar(parts[:, 1].bitcast(I32), w_raw[:].bitcast(I32), HI_BITS, None, ALU.bitwise_and)
         nc.vector.tensor_tensor(parts[:, 0], w_raw[:], parts[:, 1], ALU.subtract)
-        grouped = keep.tile([P, 2, M, PACK], BF16, name="grouped", tag="grouped", align_bytes=64)
+        grouped = keep.tile([P, 2, M, PACK], BF16, name="grouped", tag="grouped", align_bytes=256)
         nc.scalar.copy(grouped[:], parts[:].rearrange("p h j n -> p h n j"))
 
-        picked_scales = keep.tile([P, S], U8, name="picked_scales", align_bytes=64)
+        picked_scales = keep.tile([P, S], U8, name="picked_scales", align_bytes=256)
         nc.vector.tensor_copy(picked_scales[:], table_scales[:].indirect(offsets[:]))
         for q in range(4):
             first = SPREAD_FIRST + SPREAD_STEP * 4 * q
@@ -71,8 +71,8 @@ def tile_list_tabw_hl_none_kernel(tc, tab, w, offs, out):
                 picked_scales[first : first + SPREAD_STEP * 4 : SPREAD_STEP, :].bitcast(I32),
             )
 
-        codes = keep.tile([P, 2 * M], U32, name="codes", tag="shared", align_bytes=64)
-        scales = keep.tile([P, 2 * M], U8, name="scales", align_bytes=64)
+        codes = keep.tile([P, 2 * M], U32, name="codes", tag="shared", align_bytes=256)
+        scales = keep.tile([P, 2 * M], U8, name="scales", align_bytes=256)
         nc.vector.quantize_mx(
             out=codes[:].bitcast(FP8X4),
             scales=scales[:],
@@ -82,7 +82,7 @@ def tile_list_tabw_hl_none_kernel(tc, tab, w, offs, out):
         words = table_words[:].bitcast(U32)
         picked = []
         for h in range(2):
-            picked_words = keep.tile([P, HALF], U32, name="picked_words%d" % h, tag=("grouped", "second")[h], align_bytes=64)
+            picked_words = keep.tile([P, HALF], U32, name="picked_words%d" % h, tag=("grouped", "second")[h], align_bytes=256)
             cols = HALF // LANES
             nc.vector.tensor_copy(picked_words[:], words.indirect(offsets[:, h * cols : (h + 1) * cols]))
             picked.append(picked_words)
@@ -106,7 +106,7 @@ def tile_list_tabw_hl_none_kernel(tc, tab, w, offs, out):
         first = 0
         for group, width in enumerate(WIDTHS):
             bank = product(group, first, width)
-            result = keep.tile([P, width], F32, name="result%d" % group)
+            result = keep.tile([P, width], F32, name="result%d" % group, align_bytes=256)
             if first > HALF and group % 2 == 1:
                 nc.vector.tensor_copy(result[:], bank[:])
             else:

@@ -65,8 +65,7 @@ def tile_list_tabw_hl_none_kernel(tc, tab, w, offs, out):
         nc.vector.tensor_copy(picked_scales[:], table_scales[:].indirect(offsets[:]))
         for q in range(4):
             first = SPREAD_FIRST + SPREAD_STEP * 4 * q
-            queue = (nc.sync, nc.scalar)[q % 2]
-            queue.dma_start(
+            nc.sync.dma_start(
                 plane[QUADRANT * q : QUADRANT * q + 4, :].bitcast(I32),
                 picked_scales[first : first + SPREAD_STEP * 4 : SPREAD_STEP, :].bitcast(I32),
             )
@@ -107,9 +106,10 @@ def tile_list_tabw_hl_none_kernel(tc, tab, w, offs, out):
         for group, width in enumerate(WIDTHS):
             bank = product(group, first, width)
             result = keep.tile([P, width], F32, name="result%d" % group, align_bytes=256)
-            if first > HALF and group % 2 == 1:
+            if first >= HALF:
                 nc.vector.tensor_copy(result[:], bank[:])
             else:
                 nc.scalar.copy(result[:], bank[:])
-            nc.sync.dma_start(out[:, first : first + width], result[:])
+            queue = nc.scalar if first >= HALF and group % 2 == 0 else nc.sync
+            queue.dma_start(out[:, first : first + width], result[:])
             first = first + width

@@ -79,6 +79,17 @@ def tile_list_tabw_hl_none_kernel(tc, tab, w, offs, out):
         )
 
         words = table_words[:].bitcast(U32)
+        warm = psum.tile([32, HALF], F32, name="warm")
+        nc.tensor.matmul_mx(
+            out=warm[:],
+            lhsT=codes[:, :32].bitcast(FP8X4),
+            lhsT_scale=scales[:, :32],
+            rhs=words[:, T - HALF :].bitcast(FP8X4),
+            rhs_scale=picked_scales[:, :HALF],
+            start=True,
+            stop=True,
+        )
+
         picked = []
         for h in range(2):
             picked_words = keep.tile([P, HALF], U32, name="picked_words%d" % h, tag=("grouped", "second")[h], align_bytes=256)

@@ -10,7 +10,8 @@ QUARTER = S // 4
 BLOCKS = K // 32
 SPREAD_FIRST = 32
 SPREAD_STEP = 4
-FIRST = 512
+FIRST = 768
+WARM_PASSES = 6
 WIDTHS = (256, 256, 128, 128, 128, 128)
 
 FLOPS = 2 * 2 * K * M * S
@@ -36,7 +37,7 @@ def tile_list_tabw_hl_none_kernel(tc, tab, w, offs, out):
         offsets = keep.tile([P, S // LANES], U16, name="offsets", align_bytes=256)
         w_raw = keep.tile([P, PACK, M], F32, name="w_raw", align_bytes=256)
         table_words = keep.tile([P, T], I32, name="table_words", align_bytes=256)
-        table_scales = keep.tile([P, T], U8, name="table_scales", tag="shared", align_bytes=256)
+        table_scales = keep.tile([P, T], U8, name="table_scales", align_bytes=256)
         plane = keep.tile([P, S], U8, name="plane", align_bytes=256)
 
         nc.vector.memset(table_scales[:].bitcast(I32), 0)
@@ -55,11 +56,12 @@ def tile_list_tabw_hl_none_kernel(tc, tab, w, offs, out):
         )
         nc.sync.dma_start(table_words[:, FIRST:], word_rows[:, FIRST:])
 
-        parts = keep.tile([P, 2, PACK, M], F32, name="parts", align_bytes=256)
-        nc.vector.tensor_scalar(parts[:, 1].bitcast(I32), w_raw[:].bitcast(I32), HI_BITS, None, ALU.bitwise_and)
-        nc.vector.tensor_tensor(parts[:, 0], w_raw[:], parts[:, 1], ALU.subtract)
+        w_hi = keep.tile([P, PACK, M], F32, name="w_hi", align_bytes=256)
+        nc.vector.tensor_scalar(w_hi[:].bitcast(I32), w_raw[:].bitcast(I32), HI_BITS, None, ALU.bitwise_and)
+        w_side = keep.tile([P, M, PACK], F32, name="w_side", align_bytes=256)
+        nc.scalar.copy(w_side[:], w_raw[:].rearrange("p j n -> p n j"))
         grouped = keep.tile([P, 2, M, PACK], BF16, name="grouped", tag="grouped", align_bytes=256)
-        nc.scalar.copy(grouped[:], parts[:].rearrange("p h j n -> p h n j"))
+        nc.scalar.copy(grouped[:, 0], w_hi[:].rearrange("p j n -> p n j"))
 
         picked_scales = keep.tile([P, S], U8, name="picked_scales", align_bytes=256)
         nc.vector.tensor_copy(picked_scales[:], table_scales[:].indirect(offsets[:]))
@@ -70,26 +72,30 @@ def tile_list_tabw_hl_none_kernel(tc, tab, w, offs, out):
                 picked_scales[first : first + SPREAD_STEP * 4 : SPREAD_STEP, :].bitcast(I32),
             )
 
-        codes = keep.tile([P, 2 * M], U32, name="codes", tag="shared", align_bytes=256)
+        nc.vector.tensor_tensor(grouped[:, 1], w_side[:], grouped[:, 0], ALU.subtract)
+
+        codes = keep.tile([P, 2 * M], U32, name="codes", align_bytes=256)
         scales = keep.tile([P, 2 * M], U8, name="scales", align_bytes=256)
-        nc.vector.quantize_mx(
-            out=codes[:].bitcast(FP8X4),
-            scales=scales[:],
-            in_=grouped[:].rearrange("p h n j -> p (h n j)"),
-        )
+        for i in range(2):
+            nc.vector.quantize_mx(
+                out=codes[:, i * M : (i + 1) * M].bitcast(FP8X4),
+                scales=scales[:, i * M : (i + 1) * M],
+                in_=grouped[:, i].rearrange("p n j -> p (n j)"),
+            )
+
+        warm = psum.tile([32, M], F32, name="warm")
+        for step in range(WARM_PASSES):
+            nc.tensor.matmul_mx(
+                out=warm[:],
+                lhsT=codes[:, :32].bitcast(FP8X4),
+                lhsT_scale=scales[:, :32],
+                rhs=codes[:, M:].bitcast(FP8X4),
+                rhs_scale=scales[:, M:],
+                start=True,
+                stop=True,
+            )
 
         words = table_words[:].bitcast(U32)
-        warm = psum.tile([32, HALF], F32, name="warm")
-        nc.tensor.matmul_mx(
-            out=warm[:],
-            lhsT=codes[:, :32].bitcast(FP8X4),
-            lhsT_scale=scales[:, :32],
-            rhs=words[:, T - HALF :].bitcast(FP8X4),
-            rhs_scale=picked_scales[:, :HALF],
-            start=True,
-            stop=True,
-        )
-
         picked = []
         for h in range(2):
             picked_words = keep.tile([P, HALF], U32, name="picked_words%d" % h, tag=("grouped", "second")[h], align_bytes=256)

@@ -12,7 +12,7 @@ SPREAD_FIRST = 32
 SPREAD_STEP = 4
 FIRST = 768
 WARM_PASSES = 6
-WIDTHS = (256, 256, 128, 128, 128, 128)
+GROUPS = ((0, 256), (256, 256), (512, 128), (768, 128), (640, 128), (896, 128))
 
 FLOPS = 2 * 2 * K * M * S
 
@@ -119,8 +119,7 @@ def tile_list_tabw_hl_none_kernel(tc, tab, w, offs, out):
                 )
             return bank
 
-        first = 0
-        for group, width in enumerate(WIDTHS):
+        for group, (first, width) in enumerate(GROUPS):
             bank = product(group, first, width)
             result = keep.tile([P, width], F32, name="result%d" % group, align_bytes=256)
             if first >= HALF:
@@ -129,4 +128,3 @@ def tile_list_tabw_hl_none_kernel(tc, tab, w, offs, out):
                 nc.scalar.copy(result[:], bank[:])
             queue = nc.scalar if first >= HALF and group % 2 == 0 else nc.sync
             queue.dma_start(out[:, first : first + width], result[:])
-            first = first + width

@@ -5,14 +5,12 @@ P = 128
 PACK = 4
 LANES = 16
 QUADRANT = 32
-HALF = S // 2
-QUARTER = S // 4
 BLOCKS = K // 32
 SPREAD_FIRST = 32
 SPREAD_STEP = 4
 FIRST = 768
 WARM_PASSES = 6
-GROUPS = ((0, 256), (256, 256), (512, 128), (768, 128), (640, 128), (896, 128))
+PIECES = ((256,), (256,), (256,), (128, 128))
 
 FLOPS = 2 * 2 * K * M * S
 
@@ -47,7 +45,6 @@ def tile_list_tabw_hl_none_kernel(tc, tab, w, offs, out):
         nc.sync.dma_start(offsets[:], offs)
         word_rows = tab[0, : PACK * P * T].rearrange("(p b) -> p b", p=P).bitcast(I32)
         nc.sync.dma_start(table_words[:, :FIRST], word_rows[:, :FIRST])
-
         scale_rows = tab[0, PACK * P * T :].rearrange("(q t) -> q t", t=T)
         last = SPREAD_FIRST + SPREAD_STEP * BLOCKS
         nc.sync.dma_start(
@@ -97,14 +94,19 @@ def tile_list_tabw_hl_none_kernel(tc, tab, w, offs, out):
 
         words = table_words[:].bitcast(U32)
         picked = []
-        for h in range(2):
-            picked_words = keep.tile([P, HALF], U32, name="picked_words%d" % h, tag=("grouped", "second")[h], align_bytes=256)
-            cols = HALF // LANES
-            nc.vector.tensor_copy(picked_words[:], words.indirect(offsets[:, h * cols : (h + 1) * cols]))
-            picked.append(picked_words)
+        first = 0
+        for piece, groups in enumerate(PIECES):
+            width = sum(groups)
+            tag = "grouped" if piece == 0 else "picked%d" % piece
+            picked_words = keep.tile([P, width], U32, name="picked_words%d" % piece, tag=tag, align_bytes=256)
+            nc.vector.tensor_copy(picked_words[:], words.indirect(offsets[:, first // LANES : (first + width) // LANES]))
+            inside = 0
+            for group_width in groups:
+                picked.append((first + inside, group_width, picked_words[:, inside : inside + group_width]))
+                inside += group_width
+            first += width
 
-        def product(group, first, width):
-            h, inside = divmod(first, HALF)
+        for group, (first, width, moving) in enumerate(picked):
             bank = psum.tile([P, width], F32, name="bank%d" % group)
             for step in range(2):
                 i = (step + group) % 2
@@ -112,19 +114,14 @@ def tile_list_tabw_hl_none_kernel(tc, tab, w, offs, out):
                     out=bank[:],
                     lhsT=codes[:, i * M : (i + 1) * M].bitcast(FP8X4),
                     lhsT_scale=scales[:, i * M : (i + 1) * M],
-                    rhs=picked[h][:, inside : inside + width].bitcast(FP8X4),
+                    rhs=moving.bitcast(FP8X4),
                     rhs_scale=plane[:, first : first + width],
                     start=(step == 0),
                     stop=(step == 1),
                 )
-            return bank
-
-        for group, (first, width) in enumerate(GROUPS):
-            bank = product(group, first, width)
             result = keep.tile([P, width], F32, name="result%d" % group, align_bytes=256)
-            if first >= HALF:
+            if group == 3:
                 nc.vector.tensor_copy(result[:], bank[:])
             else:
                 nc.scalar.copy(result[:], bank[:])
-            queue = nc.scalar if first >= HALF and group % 2 == 0 else nc.sync
-            queue.dma_start(out[:, first : first + width], result[:])
+            nc.sync.dma_start(out[:, first : first + width], result[:])

@@ -8,9 +8,9 @@ QUADRANT = 32
 BLOCKS = K // 32
 SPREAD_FIRST = 32
 SPREAD_STEP = 4
-FIRST = 768
+FIRST = 512
 WARM_PASSES = 6
-PIECES = ((256,), (256,), (256,), (128, 128))
+PIECES = ((256,), (128, 128), (128, 128), (128, 128))
 
 FLOPS = 2 * 2 * K * M * S
 
@@ -120,7 +120,7 @@ def tile_list_tabw_hl_none_kernel(tc, tab, w, offs, out):
                     stop=(step == 1),
                 )
             result = keep.tile([P, width], F32, name="result%d" % group, align_bytes=256)
-            if group == 3:
+            if group == 5:
                 nc.vector.tensor_copy(result[:], bank[:])
             else:
                 nc.scalar.copy(result[:], bank[:])

@@ -8,7 +8,7 @@ QUADRANT = 32
 BLOCKS = K // 32
 SPREAD_FIRST = 32
 SPREAD_STEP = 4
-FIRST = 512
+FIRST = 640
 WARM_PASSES = 6
 PIECES = ((256,), (128, 128), (128, 128), (128, 128))
 
@@ -69,16 +69,15 @@ def tile_list_tabw_hl_none_kernel(tc, tab, w, offs, out):
                 picked_scales[first : first + SPREAD_STEP * 4 : SPREAD_STEP, :].bitcast(I32),
             )
 
-        nc.vector.tensor_tensor(grouped[:, 1], w_side[:], grouped[:, 0], ALU.subtract)
+        nc.gpsimd.tensor_tensor(grouped[:, 1], w_side[:], grouped[:, 0], ALU.subtract)
 
         codes = keep.tile([P, 2 * M], U32, name="codes", align_bytes=256)
         scales = keep.tile([P, 2 * M], U8, name="scales", align_bytes=256)
-        for i in range(2):
-            nc.vector.quantize_mx(
-                out=codes[:, i * M : (i + 1) * M].bitcast(FP8X4),
-                scales=scales[:, i * M : (i + 1) * M],
-                in_=grouped[:, i].rearrange("p n j -> p (n j)"),
-            )
+        nc.vector.quantize_mx(
+            out=codes[:].bitcast(FP8X4),
+            scales=scales[:],
+            in_=grouped[:].rearrange("p i n j -> p (i n j)"),
+        )
 
         warm = psum.tile([32, M], F32, name="warm")
         for step in range(WARM_PASSES):

@@ -54,11 +54,15 @@ def tile_list_tabw_hl_none_kernel(tc, tab, w, offs, out):
         nc.sync.dma_start(table_words[:, FIRST:], word_rows[:, FIRST:])
 
         w_hi = keep.tile([P, PACK, M], F32, name="w_hi", align_bytes=256)
-        nc.vector.tensor_scalar(w_hi[:].bitcast(I32), w_raw[:].bitcast(I32), HI_BITS, None, ALU.bitwise_and)
-        w_side = keep.tile([P, M, PACK], F32, name="w_side", align_bytes=256)
-        nc.scalar.copy(w_side[:], w_raw[:].rearrange("p j n -> p n j"))
-        grouped = keep.tile([P, 2, M, PACK], BF16, name="grouped", tag="grouped", align_bytes=256)
-        nc.scalar.copy(grouped[:, 0], w_hi[:].rearrange("p j n -> p n j"))
+        w_lo = keep.tile([P, PACK, M], F32, name="w_lo", align_bytes=256)
+        halves = (slice(0, PACK // 2), slice(PACK // 2, PACK))
+        for rows in halves:
+            nc.vector.tensor_scalar(w_hi[:, rows].bitcast(I32), w_raw[:, rows].bitcast(I32), HI_BITS, None, ALU.bitwise_and)
+        for rows in halves:
+            nc.vector.tensor_tensor(w_lo[:, rows], w_raw[:, rows], w_hi[:, rows], ALU.subtract)
+        grouped = keep.tile([P, 2, M, PACK], BF16, name="grouped", align_bytes=256)
+        for i, part in enumerate((w_hi, w_lo)):
+            nc.scalar.copy(grouped[:, i], part[:].rearrange("p j n -> p n j"))
 
         picked_scales = keep.tile([P, S], U8, name="picked_scales", align_bytes=256)
         nc.vector.tensor_copy(picked_scales[:], table_scales[:].indirect(offsets[:]))
@@ -69,7 +73,6 @@ def tile_list_tabw_hl_none_kernel(tc, tab, w, offs, out):
                 picked_scales[first : first + SPREAD_STEP * 4 : SPREAD_STEP, :].bitcast(I32),
             )
 
-        nc.gpsimd.tensor_tensor(grouped[:, 1], w_side[:], grouped[:, 0], ALU.subtract)
 
         codes = keep.tile([P, 2 * M], U32, name="codes", align_bytes=256)
         scales = keep.tile([P, 2 * M], U8, name="scales", align_bytes=256)
@@ -96,8 +99,7 @@ def tile_list_tabw_hl_none_kernel(tc, tab, w, offs, out):
         first = 0
         for piece, groups in enumerate(PIECES):
             width = sum(groups)
-            tag = "grouped" if piece == 0 else "picked%d" % piece
-            picked_words = keep.tile([P, width], U32, name="picked_words%d" % piece, tag=tag, align_bytes=256)
+            picked_words = keep.tile([P, width], U32, name="picked_words%d" % piece, align_bytes=256)
             nc.vector.tensor_copy(picked_words[:], words.indirect(offsets[:, first // LANES : (first + width) // LANES]))
             inside = 0
             for group_width in groups:

@@ -8,7 +8,7 @@ QUADRANT = 32
 BLOCKS = K // 32
 SPREAD_FIRST = 32
 SPREAD_STEP = 4
-FIRST = 640
+FIRST = 512
 WARM_PASSES = 6
 PIECES = ((256,), (128, 128), (128, 128), (128, 128))
 
@@ -44,7 +44,8 @@ def tile_list_tabw_hl_none_kernel(tc, tab, w, offs, out):
         nc.sync.dma_start(w_raw[:], w.rearrange("(p j) n -> p j n", j=PACK))
         nc.sync.dma_start(offsets[:], offs)
         word_rows = tab[0, : PACK * P * T].rearrange("(p b) -> p b", p=P).bitcast(I32)
-        nc.sync.dma_start(table_words[:, :FIRST], word_rows[:, :FIRST])
+        head = keep.tile([P, FIRST], I32, name="head", align_bytes=256)
+        nc.sync.dma_start(head[:], word_rows[:, :FIRST])
         scale_rows = tab[0, PACK * P * T :].rearrange("(q t) -> q t", t=T)
         last = SPREAD_FIRST + SPREAD_STEP * BLOCKS
         nc.sync.dma_start(
@@ -54,15 +55,17 @@ def tile_list_tabw_hl_none_kernel(tc, tab, w, offs, out):
         nc.sync.dma_start(table_words[:, FIRST:], word_rows[:, FIRST:])
 
         w_hi = keep.tile([P, PACK, M], F32, name="w_hi", align_bytes=256)
-        w_lo = keep.tile([P, PACK, M], F32, name="w_lo", align_bytes=256)
-        halves = (slice(0, PACK // 2), slice(PACK // 2, PACK))
-        for rows in halves:
-            nc.vector.tensor_scalar(w_hi[:, rows].bitcast(I32), w_raw[:, rows].bitcast(I32), HI_BITS, None, ALU.bitwise_and)
-        for rows in halves:
-            nc.vector.tensor_tensor(w_lo[:, rows], w_raw[:, rows], w_hi[:, rows], ALU.subtract)
+        early, late = slice(0, M // 2), slice(M // 2, M)
+        for cols in (early, late):
+            nc.vector.tensor_scalar(w_hi[:, :, cols].bitcast(I32), w_raw[:, :, cols].bitcast(I32), HI_BITS, None, ALU.bitwise_and)
+        w_lo_early = keep.tile([P, PACK, M // 2], F32, name="w_lo_early", align_bytes=256)
+        nc.vector.tensor_tensor(w_lo_early[:], w_raw[:, :, early], w_hi[:, :, early], ALU.subtract)
+        nc.vector.tensor_copy(table_words[:, :FIRST], head[:])
+        w_late = keep.tile([P, M // 2, PACK], F32, name="w_late", align_bytes=256)
+        nc.scalar.copy(w_late[:], w_raw[:, :, late].rearrange("p j n -> p n j"))
         grouped = keep.tile([P, 2, M, PACK], BF16, name="grouped", align_bytes=256)
-        for i, part in enumerate((w_hi, w_lo)):
-            nc.scalar.copy(grouped[:, i], part[:].rearrange("p j n -> p n j"))
+        nc.scalar.copy(grouped[:, 1, early], w_lo_early[:].rearrange("p j n -> p n j"))
+        nc.scalar.copy(grouped[:, 0], w_hi[:].rearrange("p j n -> p n j"))
 
         picked_scales = keep.tile([P, S], U8, name="picked_scales", align_bytes=256)
         nc.vector.tensor_copy(picked_scales[:], table_scales[:].indirect(offsets[:]))
@@ -73,14 +76,16 @@ def tile_list_tabw_hl_none_kernel(tc, tab, w, offs, out):
                 picked_scales[first : first + SPREAD_STEP * 4 : SPREAD_STEP, :].bitcast(I32),
             )
 
+        nc.vector.tensor_tensor(grouped[:, 1, late], w_late[:], grouped[:, 0, late], ALU.subtract)
 
         codes = keep.tile([P, 2 * M], U32, name="codes", align_bytes=256)
         scales = keep.tile([P, 2 * M], U8, name="scales", align_bytes=256)
-        nc.vector.quantize_mx(
-            out=codes[:].bitcast(FP8X4),
-            scales=scales[:],
-            in_=grouped[:].rearrange("p i n j -> p (i n j)"),
-        )
+        for i in range(2):
+            nc.vector.quantize_mx(
+                out=codes[:, i * M : (i + 1) * M].bitcast(FP8X4),
+                scales=scales[:, i * M : (i + 1) * M],
+                in_=grouped[:, i].rearrange("p n j -> p (n j)"),
+            )
 
         warm = psum.tile([32, M], F32, name="warm")
         for step in range(WARM_PASSES):

@@ -10,7 +10,8 @@ SPREAD_FIRST = 32
 SPREAD_STEP = 4
 FIRST = 512
 WARM_PASSES = 6
-PIECES = ((256,), (128, 128), (128, 128), (128, 128))
+PIECES = ((128, 128),) * 4
+STORES = (128, 128, 128, 128, 128, 128, 256)
 
 FLOPS = 2 * 2 * K * M * S
 
@@ -87,7 +88,7 @@ def tile_list_tabw_hl_none_kernel(tc, tab, w, offs, out):
                 in_=grouped[:, i].rearrange("p n j -> p (n j)"),
             )
 
-        warm = psum.tile([32, M], F32, name="warm")
+        warm = psum.tile([32, M], F32, name="warm", tag="bank7")
         for step in range(WARM_PASSES):
             nc.tensor.matmul_mx(
                 out=warm[:],
@@ -112,8 +113,10 @@ def tile_list_tabw_hl_none_kernel(tc, tab, w, offs, out):
                 inside += group_width
             first += width
 
+        results = [keep.tile([P, width], F32, name="result%d" % i, align_bytes=256) for i, width in enumerate(STORES)]
+        store, filled = 0, 0
         for group, (first, width, moving) in enumerate(picked):
-            bank = psum.tile([P, width], F32, name="bank%d" % group)
+            bank = psum.tile([P, width], F32, name="bank%d" % group, tag="bank%d" % group)
             for step in range(2):
                 i = (step + group) % 2
                 nc.tensor.matmul_mx(
@@ -125,9 +128,12 @@ def tile_list_tabw_hl_none_kernel(tc, tab, w, offs, out):
                     start=(step == 0),
                     stop=(step == 1),
                 )
-            result = keep.tile([P, width], F32, name="result%d" % group, align_bytes=256)
-            if group == 5:
-                nc.vector.tensor_copy(result[:], bank[:])
+            target = results[store][:, filled : filled + width]
+            if first >= S - 256:
+                nc.vector.tensor_copy(target, bank[:])
             else:
-                nc.scalar.copy(result[:], bank[:])
-            nc.sync.dma_start(out[:, first : first + width], result[:])
+                nc.scalar.copy(target, bank[:])
+            filled += width
+            if filled == STORES[store]:
+                nc.sync.dma_start(out[:, first + width - filled : first + width], results[store][:])
+                store, filled = store + 1, 0

@@ -8,9 +8,9 @@ QUADRANT = 32
 BLOCKS = K // 32
 SPREAD_FIRST = 32
 SPREAD_STEP = 4
-FIRST = 512
 WARM_PASSES = 6
-PIECES = ((128, 128),) * 4
+PIECE = 256
+GROUP = 128
 STORES = (128, 128, 128, 128, 128, 128, 256)
 
 FLOPS = 2 * 2 * K * M * S
@@ -31,62 +31,53 @@ def tile_list_tabw_hl_none_kernel(tc, tab, w, offs, out):
     nc = tc.nc
     with (
         tc.tile_pool(name="keep", bufs=1) as keep,
+        tc.tile_pool(name="shared", bufs=1) as shared,
         tc.psum_pool(name="psum", bufs=1) as psum,
     ):
         offsets = keep.tile([P, S // LANES], U16, name="offsets", align_bytes=256)
         w_raw = keep.tile([P, PACK, M], F32, name="w_raw", align_bytes=256)
         table_words = keep.tile([P, T], I32, name="table_words", align_bytes=256)
-        table_scales = keep.tile([P, T], U8, name="table_scales", align_bytes=256)
         plane = keep.tile([P, S], U8, name="plane", align_bytes=256)
+        table_scales = shared.tile([P, T], U8, name="table_scales", align_bytes=256, offset=0)
 
         nc.vector.memset(table_scales[:].bitcast(I32), 0)
         nc.vector.memset(plane[:].bitcast(I32), 0)
 
         nc.sync.dma_start(w_raw[:], w.rearrange("(p j) n -> p j n", j=PACK))
         nc.sync.dma_start(offsets[:], offs)
-        word_rows = tab[0, : PACK * P * T].rearrange("(p b) -> p b", p=P).bitcast(I32)
-        head = keep.tile([P, FIRST], I32, name="head", align_bytes=256)
-        nc.sync.dma_start(head[:], word_rows[:, :FIRST])
         scale_rows = tab[0, PACK * P * T :].rearrange("(q t) -> q t", t=T)
         last = SPREAD_FIRST + SPREAD_STEP * BLOCKS
         nc.sync.dma_start(
             table_scales[SPREAD_FIRST:last:SPREAD_STEP, :].bitcast(I32),
             scale_rows.bitcast(I32),
         )
-        nc.sync.dma_start(table_words[:, FIRST:], word_rows[:, FIRST:])
+        word_rows = tab[0, : PACK * P * T].rearrange("(p b) -> p b", p=P).bitcast(I32)
+        nc.scalar.dma_start(table_words[:], word_rows)
 
         w_hi = keep.tile([P, PACK, M], F32, name="w_hi", align_bytes=256)
-        early, late = slice(0, M // 2), slice(M // 2, M)
-        for cols in (early, late):
-            nc.vector.tensor_scalar(w_hi[:, :, cols].bitcast(I32), w_raw[:, :, cols].bitcast(I32), HI_BITS, None, ALU.bitwise_and)
-        w_lo_early = keep.tile([P, PACK, M // 2], F32, name="w_lo_early", align_bytes=256)
-        nc.vector.tensor_tensor(w_lo_early[:], w_raw[:, :, early], w_hi[:, :, early], ALU.subtract)
-        nc.vector.tensor_copy(table_words[:, :FIRST], head[:])
-        w_late = keep.tile([P, M // 2, PACK], F32, name="w_late", align_bytes=256)
-        nc.scalar.copy(w_late[:], w_raw[:, :, late].rearrange("p j n -> p n j"))
-        grouped = keep.tile([P, 2, M, PACK], BF16, name="grouped", align_bytes=256)
-        nc.scalar.copy(grouped[:, 1, early], w_lo_early[:].rearrange("p j n -> p n j"))
+        w_lo = keep.tile([P, PACK, M], F32, name="w_lo", align_bytes=256)
+        nc.vector.tensor_scalar(w_hi[:].bitcast(I32), w_raw[:].bitcast(I32), HI_BITS, None, ALU.bitwise_and)
+        nc.vector.tensor_tensor(w_lo[:], w_raw[:], w_hi[:], ALU.subtract)
+        grouped = shared.tile([P, 2, M, PACK], BF16, name="grouped", align_bytes=256, offset=T)
         nc.scalar.copy(grouped[:, 0], w_hi[:].rearrange("p j n -> p n j"))
+        nc.scalar.copy(grouped[:, 1], w_lo[:].rearrange("p j n -> p n j"))
 
         picked_scales = keep.tile([P, S], U8, name="picked_scales", align_bytes=256)
         nc.vector.tensor_copy(picked_scales[:], table_scales[:].indirect(offsets[:]))
         for q in range(4):
             first = SPREAD_FIRST + SPREAD_STEP * 4 * q
-            nc.sync.dma_start(
+            nc.scalar.dma_start(
                 plane[QUADRANT * q : QUADRANT * q + 4, :].bitcast(I32),
                 picked_scales[first : first + SPREAD_STEP * 4 : SPREAD_STEP, :].bitcast(I32),
             )
 
-        nc.vector.tensor_tensor(grouped[:, 1, late], w_late[:], grouped[:, 0, late], ALU.subtract)
-
-        codes = keep.tile([P, 2 * M], U32, name="codes", align_bytes=256)
+        codes = shared.tile([P, 2 * M], U32, name="codes", align_bytes=256, offset=0)
         scales = keep.tile([P, 2 * M], U8, name="scales", align_bytes=256)
-        for i in range(2):
-            nc.vector.quantize_mx(
-                out=codes[:, i * M : (i + 1) * M].bitcast(FP8X4),
-                scales=scales[:, i * M : (i + 1) * M],
-                in_=grouped[:, i].rearrange("p n j -> p (n j)"),
-            )
+        nc.vector.quantize_mx(
+            out=codes[:].bitcast(FP8X4),
+            scales=scales[:],
+            in_=grouped[:].rearrange("p i n j -> p (i n j)"),
+        )
 
         warm = psum.tile([32, M], F32, name="warm", tag="bank7")
         for step in range(WARM_PASSES):
@@ -101,39 +92,34 @@ def tile_list_tabw_hl_none_kernel(tc, tab, w, offs, out):
             )
 
         words = table_words[:].bitcast(U32)
-        picked = []
-        first = 0
-        for piece, groups in enumerate(PIECES):
-            width = sum(groups)
-            picked_words = keep.tile([P, width], U32, name="picked_words%d" % piece, align_bytes=256)
-            nc.vector.tensor_copy(picked_words[:], words.indirect(offsets[:, first // LANES : (first + width) // LANES]))
-            inside = 0
-            for group_width in groups:
-                picked.append((first + inside, group_width, picked_words[:, inside : inside + group_width]))
-                inside += group_width
-            first += width
+        picked_words = shared.tile([P, S], U32, name="picked_words", align_bytes=256, offset=T // 2)
+        for first in range(0, S, PIECE):
+            nc.vector.tensor_copy(
+                picked_words[:, first : first + PIECE],
+                words.indirect(offsets[:, first // LANES : (first + PIECE) // LANES]),
+            )
 
         results = [keep.tile([P, width], F32, name="result%d" % i, align_bytes=256) for i, width in enumerate(STORES)]
         store, filled = 0, 0
-        for group, (first, width, moving) in enumerate(picked):
-            bank = psum.tile([P, width], F32, name="bank%d" % group, tag="bank%d" % group)
+        for group, first in enumerate(range(0, S, GROUP)):
+            bank = psum.tile([P, GROUP], F32, name="bank%d" % group, tag="bank%d" % group)
             for step in range(2):
                 i = (step + group) % 2
                 nc.tensor.matmul_mx(
                     out=bank[:],
                     lhsT=codes[:, i * M : (i + 1) * M].bitcast(FP8X4),
                     lhsT_scale=scales[:, i * M : (i + 1) * M],
-                    rhs=moving.bitcast(FP8X4),
-                    rhs_scale=plane[:, first : first + width],
+                    rhs=picked_words[:, first : first + GROUP].bitcast(FP8X4),
+                    rhs_scale=plane[:, first : first + GROUP],
                     start=(step == 0),
                     stop=(step == 1),
                 )
-            target = results[store][:, filled : filled + width]
-            if first >= S - 256:
+            target = results[store][:, filled : filled + GROUP]
+            if first >= S - PIECE:
                 nc.vector.tensor_copy(target, bank[:])
             else:
                 nc.scalar.copy(target, bank[:])
-            filled += width
+            filled += GROUP
             if filled == STORES[store]:
-                nc.sync.dma_start(out[:, first + width - filled : first + width], results[store][:])
+                nc.sync.dma_start(out[:, first + GROUP - filled : first + GROUP], results[store][:])
                 store, filled = store + 1, 0

@@ -10,8 +10,10 @@ SPREAD_FIRST = 32
 SPREAD_STEP = 4
 WARM_PASSES = 6
 PIECE = 256
+FIRST = 512
+HALF = S // 2
 GROUP = 128
-STORES = (128, 128, 128, 128, 128, 128, 256)
+STORES = (128,) * 8
 
 FLOPS = 2 * 2 * K * M * S
 
@@ -45,31 +47,39 @@ def tile_list_tabw_hl_none_kernel(tc, tab, w, offs, out):
 
         nc.sync.dma_start(w_raw[:], w.rearrange("(p j) n -> p j n", j=PACK))
         nc.sync.dma_start(offsets[:], offs)
+        word_rows = tab[0, : PACK * P * T].rearrange("(p b) -> p b", p=P).bitcast(I32)
+        head = keep.tile([P, FIRST], I32, name="head", align_bytes=256)
+        nc.sync.dma_start(head[:], word_rows[:, :FIRST])
         scale_rows = tab[0, PACK * P * T :].rearrange("(q t) -> q t", t=T)
         last = SPREAD_FIRST + SPREAD_STEP * BLOCKS
         nc.sync.dma_start(
             table_scales[SPREAD_FIRST:last:SPREAD_STEP, :].bitcast(I32),
             scale_rows.bitcast(I32),
         )
-        word_rows = tab[0, : PACK * P * T].rearrange("(p b) -> p b", p=P).bitcast(I32)
-        nc.scalar.dma_start(table_words[:], word_rows)
+        nc.sync.dma_start(table_words[:, FIRST:], word_rows[:, FIRST:])
 
         w_hi = keep.tile([P, PACK, M], F32, name="w_hi", align_bytes=256)
         w_lo = keep.tile([P, PACK, M], F32, name="w_lo", align_bytes=256)
         nc.vector.tensor_scalar(w_hi[:].bitcast(I32), w_raw[:].bitcast(I32), HI_BITS, None, ALU.bitwise_and)
         nc.vector.tensor_tensor(w_lo[:], w_raw[:], w_hi[:], ALU.subtract)
-        grouped = shared.tile([P, 2, M, PACK], BF16, name="grouped", align_bytes=256, offset=T)
+        nc.vector.tensor_copy(table_words[:, :FIRST], head[:])
+        grouped = keep.tile([P, 2, M, PACK], BF16, name="grouped", align_bytes=256)
         nc.scalar.copy(grouped[:, 0], w_hi[:].rearrange("p j n -> p n j"))
         nc.scalar.copy(grouped[:, 1], w_lo[:].rearrange("p j n -> p n j"))
 
-        picked_scales = keep.tile([P, S], U8, name="picked_scales", align_bytes=256)
-        nc.vector.tensor_copy(picked_scales[:], table_scales[:].indirect(offsets[:]))
-        for q in range(4):
-            first = SPREAD_FIRST + SPREAD_STEP * 4 * q
-            nc.scalar.dma_start(
-                plane[QUADRANT * q : QUADRANT * q + 4, :].bitcast(I32),
-                picked_scales[first : first + SPREAD_STEP * 4 : SPREAD_STEP, :].bitcast(I32),
+        for half in range(2):
+            columns = slice(half * HALF, (half + 1) * HALF)
+            picked_scales = keep.tile([P, HALF], U8, name="picked_scales%d" % half, align_bytes=256)
+            nc.vector.tensor_copy(
+                picked_scales[:],
+                table_scales[:].indirect(offsets[:, columns.start // LANES : columns.stop // LANES]),
             )
+            for q in range(4):
+                first = SPREAD_FIRST + SPREAD_STEP * 4 * q
+                nc.sync.dma_start(
+                    plane[QUADRANT * q : QUADRANT * q + 4, columns].bitcast(I32),
+                    picked_scales[first : first + SPREAD_STEP * 4 : SPREAD_STEP, :].bitcast(I32),
+                )
 
         codes = shared.tile([P, 2 * M], U32, name="codes", align_bytes=256, offset=0)
         scales = keep.tile([P, 2 * M], U8, name="scales", align_bytes=256)
@@ -92,15 +102,14 @@ def tile_list_tabw_hl_none_kernel(tc, tab, w, offs, out):
             )
 
         words = table_words[:].bitcast(U32)
-        picked_words = shared.tile([P, S], U32, name="picked_words", align_bytes=256, offset=T // 2)
+        picked_words = keep.tile([P, S], U32, name="picked_words", align_bytes=256)
         for first in range(0, S, PIECE):
             nc.vector.tensor_copy(
                 picked_words[:, first : first + PIECE],
                 words.indirect(offsets[:, first // LANES : (first + PIECE) // LANES]),
             )
 
-        results = [keep.tile([P, width], F32, name="result%d" % i, align_bytes=256) for i, width in enumerate(STORES)]
-        store, filled = 0, 0
+        store = 0
         for group, first in enumerate(range(0, S, GROUP)):
             bank = psum.tile([P, GROUP], F32, name="bank%d" % group, tag="bank%d" % group)
             for step in range(2):
@@ -114,12 +123,14 @@ def tile_list_tabw_hl_none_kernel(tc, tab, w, offs, out):
                     start=(step == 0),
                     stop=(step == 1),
                 )
-            target = results[store][:, filled : filled + GROUP]
+            result = keep.tile([P, GROUP], F32, name="result%d" % group, align_bytes=256)
             if first >= S - PIECE:
-                nc.vector.tensor_copy(target, bank[:])
+                nc.vector.tensor_copy(result[:], bank[:])
             else:
-                nc.scalar.copy(target, bank[:])
-            filled += GROUP
-            if filled == STORES[store]:
-                nc.sync.dma_start(out[:, first + GROUP - filled : first + GROUP], results[store][:])
-                store, filled = store + 1, 0
+                nc.scalar.copy(result[:], bank[:])
+            inside = 0
+            while inside < GROUP:
+                width = STORES[store]
+                nc.sync.dma_start(out[:, first + inside : first + inside + width], result[:, inside : inside + width])
+                inside += width
+                store += 1

@@ -74,11 +74,14 @@ def tile_list_tabw_hl_none_kernel(tc, tab, w, offs, out):
                 picked_scales[:],
                 table_scales[:].indirect(offsets[:, columns.start // LANES : columns.stop // LANES]),
             )
-            for q in range(4):
+            moves = [(q, 0, HALF) for q in range(4)]
+            if half == 1:
+                moves = moves[:2] + [(q, inside, PIECE) for inside in (0, PIECE) for q in (2, 3)]
+            for q, inside, width in moves:
                 first = SPREAD_FIRST + SPREAD_STEP * 4 * q
                 nc.sync.dma_start(
-                    plane[QUADRANT * q : QUADRANT * q + 4, columns].bitcast(I32),
-                    picked_scales[first : first + SPREAD_STEP * 4 : SPREAD_STEP, :].bitcast(I32),
+                    plane[QUADRANT * q : QUADRANT * q + 4, columns.start + inside : columns.start + inside + width].bitcast(I32),
+                    picked_scales[first : first + SPREAD_STEP * 4 : SPREAD_STEP, inside : inside + width].bitcast(I32),
                 )
 
         codes = shared.tile([P, 2 * M], U32, name="codes", align_bytes=256, offset=0)

@@ -54,7 +54,7 @@ def tile_list_tabw_hl_none_kernel(tc, tab, w, offs, out):
         last = SPREAD_FIRST + SPREAD_STEP * BLOCKS
         nc.sync.dma_start(
             table_scales[SPREAD_FIRST:last:SPREAD_STEP, :].bitcast(I32),
-            scale_rows.bitcast(I32),
+            scale_rows.rearrange("(j o) t -> o j t", j=2).bitcast(I32),
         )
         nc.sync.dma_start(table_words[:, FIRST:], word_rows[:, FIRST:])
 
@@ -78,10 +78,10 @@ def tile_list_tabw_hl_none_kernel(tc, tab, w, offs, out):
             if half == 1:
                 moves = moves[:2] + [(q, inside, PIECE) for inside in (0, PIECE) for q in (2, 3)]
             for q, inside, width in moves:
-                first = SPREAD_FIRST + SPREAD_STEP * 4 * q
+                first = SPREAD_FIRST + QUADRANT * (q % 2) + SPREAD_STEP * (q // 2)
                 nc.sync.dma_start(
                     plane[QUADRANT * q : QUADRANT * q + 4, columns.start + inside : columns.start + inside + width].bitcast(I32),
-                    picked_scales[first : first + SPREAD_STEP * 4 : SPREAD_STEP, inside : inside + width].bitcast(I32),
+                    picked_scales[first : first + QUADRANT - SPREAD_STEP : 2 * SPREAD_STEP, inside : inside + width].bitcast(I32),
                 )
 
         codes = shared.tile([P, 2 * M], U32, name="codes", align_bytes=256, offset=0)

import concourse.mybir as mybir

K, M, T, S = 512, 128, 4096, 1024
P = 128
PACK = 4
LANES = 16
QUADRANT = 32
BLOCKS = K // 32
SPREAD_FIRST = 32
SPREAD_STEP = 4
WARM_PASSES = 6
PIECE = 256
FIRST = 512
HALF = S // 2
GROUP = 128
STORES = (128,) * 8

FLOPS = 2 * 2 * K * M * S

F32 = mybir.dt.float32
BF16 = mybir.dt.bfloat16
I32 = mybir.dt.int32
U32 = mybir.dt.uint32
U16 = mybir.dt.uint16
U8 = mybir.dt.uint8
FP8X4 = mybir.dt.float8_e4m3fn_x4
ALU = mybir.AluOpType

HI_BITS = -(1 << 20)


def tile_list_tabw_hl_none_kernel(tc, tab, w, offs, out):
    nc = tc.nc
    with (
        tc.tile_pool(name="keep", bufs=1) as keep,
        tc.tile_pool(name="shared", bufs=1) as shared,
        tc.psum_pool(name="psum", bufs=1) as psum,
    ):
        offsets = keep.tile([P, S // LANES], U16, name="offsets", align_bytes=256)
        w_raw = keep.tile([P, PACK, M], F32, name="w_raw", align_bytes=256)
        table_words = keep.tile([P, T], I32, name="table_words", align_bytes=256)
        plane = keep.tile([P, S], U8, name="plane", align_bytes=256)
        table_scales = shared.tile([P, T], U8, name="table_scales", align_bytes=256, offset=0)

        nc.vector.memset(table_scales[:].bitcast(I32), 0)
        nc.vector.memset(plane[:].bitcast(I32), 0)

        nc.sync.dma_start(w_raw[:], w.rearrange("(p j) n -> p j n", j=PACK))
        nc.sync.dma_start(offsets[:], offs)
        word_rows = tab[0, : PACK * P * T].rearrange("(p b) -> p b", p=P).bitcast(I32)
        head = keep.tile([P, FIRST], I32, name="head", align_bytes=256)
        nc.sync.dma_start(head[:], word_rows[:, :FIRST])
        scale_rows = tab[0, PACK * P * T :].rearrange("(q t) -> q t", t=T)
        last = SPREAD_FIRST + SPREAD_STEP * BLOCKS
        nc.sync.dma_start(
            table_scales[SPREAD_FIRST:last:SPREAD_STEP, :].bitcast(I32),
            scale_rows.rearrange("(j o) t -> o j t", j=2).bitcast(I32),
        )
        nc.sync.dma_start(table_words[:, FIRST:], word_rows[:, FIRST:])

        w_hi = keep.tile([P, PACK, M], F32, name="w_hi", align_bytes=256)
        w_lo = keep.tile([P, PACK, M], F32, name="w_lo", align_bytes=256)
        nc.vector.tensor_scalar(w_hi[:].bitcast(I32), w_raw[:].bitcast(I32), HI_BITS, None, ALU.bitwise_and)
        nc.vector.tensor_tensor(w_lo[:], w_raw[:], w_hi[:], ALU.subtract)
        nc.vector.tensor_copy(table_words[:, :FIRST], head[:])
        grouped = keep.tile([P, 2, M, PACK], BF16, name="grouped", align_bytes=256)
        nc.scalar.copy(grouped[:, 0], w_hi[:].rearrange("p j n -> p n j"))
        nc.scalar.copy(grouped[:, 1], w_lo[:].rearrange("p j n -> p n j"))

        for half in range(2):
            columns = slice(half * HALF, (half + 1) * HALF)
            picked_scales = keep.tile([P, HALF], U8, name="picked_scales%d" % half, align_bytes=256)
            nc.vector.tensor_copy(
                picked_scales[:],
                table_scales[:].indirect(offsets[:, columns.start // LANES : columns.stop // LANES]),
            )
            moves = [(q, 0, HALF) for q in range(4)]
            if half == 1:
                moves = moves[:2] + [(q, inside, PIECE) for inside in (0, PIECE) for q in (2, 3)]
            for q, inside, width in moves:
                first = SPREAD_FIRST + QUADRANT * (q % 2) + SPREAD_STEP * (q // 2)
                nc.sync.dma_start(
                    plane[QUADRANT * q : QUADRANT * q + 4, columns.start + inside : columns.start + inside + width].bitcast(I32),
                    picked_scales[first : first + QUADRANT - SPREAD_STEP : 2 * SPREAD_STEP, inside : inside + width].bitcast(I32),
                )

        codes = shared.tile([P, 2 * M], U32, name="codes", align_bytes=256, offset=0)
        scales = keep.tile([P, 2 * M], U8, name="scales", align_bytes=256)
        nc.vector.quantize_mx(
            out=codes[:].bitcast(FP8X4),
            scales=scales[:],
            in_=grouped[:].rearrange("p i n j -> p (i n j)"),
        )

        warm = psum.tile([32, M], F32, name="warm", tag="bank7")
        for step in range(WARM_PASSES):
            nc.tensor.matmul_mx(
                out=warm[:],
                lhsT=codes[:, :32].bitcast(FP8X4),
                lhsT_scale=scales[:, :32],
                rhs=codes[:, M:].bitcast(FP8X4),
                rhs_scale=scales[:, M:],
                start=True,
                stop=True,
            )

        words = table_words[:].bitcast(U32)
        picked_words = keep.tile([P, S], U32, name="picked_words", align_bytes=256)
        for first in range(0, S, PIECE):
            nc.vector.tensor_copy(
                picked_words[:, first : first + PIECE],
                words.indirect(offsets[:, first // LANES : (first + PIECE) // LANES]),
            )

        store = 0
        for group, first in enumerate(range(0, S, GROUP)):
            bank = psum.tile([P, GROUP], F32, name="bank%d" % group, tag="bank%d" % group)
            for step in range(2):
                i = (step + group) % 2
                nc.tensor.matmul_mx(
                    out=bank[:],
                    lhsT=codes[:, i * M : (i + 1) * M].bitcast(FP8X4),
                    lhsT_scale=scales[:, i * M : (i + 1) * M],
                    rhs=picked_words[:, first : first + GROUP].bitcast(FP8X4),
                    rhs_scale=plane[:, first : first + GROUP],
                    start=(step == 0),
                    stop=(step == 1),
                )
            result = keep.tile([P, GROUP], F32, name="result%d" % group, align_bytes=256)
            if first >= S - PIECE:
                nc.vector.tensor_copy(result[:], bank[:])
            else:
                nc.scalar.copy(result[:], bank[:])
            inside = 0
            while inside < GROUP:
                width = STORES[store]
                nc.sync.dma_start(out[:, first + inside : first + inside + width], result[:, inside : inside + width])
                inside += width
                store += 1
